import numpy as np
import ml_dtypes


def mxq(x, axis, fmt="e4m3"):
    dtype, down = {"e4m3": (ml_dtypes.float8_e4m3fn, 7), "e5m2": (ml_dtypes.float8_e5m2, 14)}[fmt]
    v = np.moveaxis(np.asarray(x, np.float32).astype(ml_dtypes.bfloat16).astype(np.float64), axis, -1)
    blocks = v.reshape(v.shape[:-1] + (-1, 32))
    amax = np.abs(blocks).max(-1, keepdims=True)
    byte = np.maximum(np.where(amax > 0, np.frexp(amax)[1] - 1 + 127, 0) - down, 1)
    scale = np.exp2(byte - 127.0)
    codes = (blocks / scale).astype(np.float32).astype(dtype).astype(np.float64)
    return np.moveaxis((codes * scale).reshape(v.shape), -1, axis)


WIDE = False


def mx_kscale(k):
    if not WIDE:
        return np.ones(k)
    levels = np.array([30, -30])
    if k % 512:
        return np.exp2(np.random.permutation(np.resize(levels, k // 32))).repeat(32)
    a = np.empty((k // 512, 16))
    for p in range(k // 512):
        a[p, :8] = np.random.permutation(np.resize(levels, 8))
        for g in range(8):
            far = levels[np.abs(levels - a[p, g]) >= 10]
            a[p, g + 8] = far[np.random.randint(len(far))]
    return np.exp2(a.ravel()).repeat(32)


BF16 = ml_dtypes.bfloat16


def bf(x):
    return np.asarray(x, np.float32).astype(BF16)


def f64(x):
    return np.asarray(x).astype(np.float64)


E2M1 = np.array([0.0, 0.5, 1.0, 1.5, 2.0, 3.0, 4.0, 6.0, -0.0, -0.5, -1.0, -1.5, -2.0, -3.0, -4.0, -6.0])


def pack_weight(w, fmt):
    k, n = w.shape
    w = f64(bf(w)).reshape(k // 32, 32, n)
    amax = np.abs(w).max(1)
    if fmt in ("e4m3", "e5m2"):
        byte = np.frexp(amax)[1] - 1 + 127 - (7 if fmt == "e4m3" else 14)
    else:
        mant, ex = np.frexp(amax / 6.0)
        byte = np.where(mant > 0.5, ex, ex - 1) + 127
    byte = np.clip(np.where(amax > 0, byte, 1), 1, 254)
    scaled = (w * np.exp2(127.0 - byte)[:, None, :]).reshape(k, n).astype(np.float32)
    by_word = np.ascontiguousarray(scaled.reshape(k // 512, 128, 4, n).transpose(0, 1, 3, 2))
    if fmt in ("e4m3", "e5m2"):
        words = by_word.astype(ml_dtypes.float8_e4m3fn if fmt == "e4m3" else ml_dtypes.float8_e5m2).view(np.uint8)
    else:
        c = by_word.astype(ml_dtypes.float4_e2m1fn).view(np.uint8) & 0xF
        words = c[..., 0::2] | (c[..., 1::2] << 4)
    return np.ascontiguousarray(words), np.ascontiguousarray(byte.astype(np.uint8).reshape(k // 512, 16, n))


def unpack_weight(words, scales, fmt):
    g, p, n, _ = words.shape
    if fmt in ("e4m3", "e5m2"):
        vals = np.ascontiguousarray(words).view(ml_dtypes.float8_e4m3fn if fmt == "e4m3" else ml_dtypes.float8_e5m2).astype(np.float64)
    else:
        nib = np.empty((g, p, n, 4), np.uint8)
        nib[..., 0::2] = words & 0xF
        nib[..., 1::2] = words >> 4
        vals = E2M1[nib]
    vals = vals * np.repeat(np.exp2(scales.astype(np.float64) - 127.0), 8, axis=1)[..., None]
    return vals.transpose(0, 1, 3, 2).reshape(g * 512, n)


C, R, Q = 1024, 2048, 1536

H = 0.5


def setup_inputs():
    s = mx_kscale(C)
    u = mx_kscale(R)
    spread = np.exp(np.random.standard_normal((C, C)) - 1.0)
    G = np.random.standard_normal((C, C)) * spread / np.sqrt(C) / s[:, None]
    jac_words, jac_scales = pack_weight(G, "e5m2")
    return {"jac_words": jac_words,
            "jac_scales": jac_scales,
            "sens": bf(np.random.standard_normal((C, Q)) * s[:, None]),
            "unit": bf(np.exp(0.3 * np.random.standard_normal(C)) / s),
            "nu": bf(np.random.standard_normal((C, R)) / np.sqrt(R) * u),
            "drdp": bf(np.random.standard_normal((R, Q)) / u[:, None])}


def reference(jac_words, jac_scales, sens, unit, nu, drdp):
    G = unpack_weight(jac_words, jac_scales, "e5m2")
    through_y = G.T @ mxq(f64(sens), 0, "e4m3")
    through_r = mxq(f64(nu), 1, "e4m3") @ mxq(f64(drdp), 0, "e4m3")
    rate = through_y + through_r
    return f64(unit)[:, None] * f64(sens) + H * rate

from contextlib import ExitStack

import concourse.mybir as mybir
from concourse.masks import make_identity

F32 = mybir.dt.float32
BF16 = mybir.dt.bfloat16
I32 = mybir.dt.int32
U8 = mybir.dt.uint8
E4M3 = mybir.dt.float8_e4m3fn_x4
E5M2 = mybir.dt.float8_e5m2_x4
ACT = mybir.ActivationFunctionType
ALU = mybir.AluOpType

C, R, Q = 1024, 2048, 1536
FLOPS = 2 * C * Q * (C + R)

P = 128
W = 512
GS, GD = C // 512, R // 512
M = C // P
OPEN = 6
ITEMS1 = [
    ("nu", 0), ("G", 0), ("s", 0, 0), ("nu", 1), ("nu", 2), ("s", 1, 0), ("nu", 3), ("nu", 4), ("G", 1), ("d", 0, 0), ("nu", 5), ("d", 1, 0), ("nu", 6), ("d", 3, 0), ("d", 2, 0), ("nu", 7)
]
V_S0 = 192
V_D0 = 256
SPLIT0 = 2
S_BANKS = (0,)
V_WIDE = 160


def tile_kinetics_sensitivity_step_e4_kernel(tc, jac_words, jac_scales, sens, unit, nu, drdp, out):
    nc = tc.nc
    with ExitStack() as ctx:
        keep = ctx.enter_context(tc.tile_pool(name="keep", bufs=1))
        stage = ctx.enter_context(tc.tile_pool(name="stage", bufs=6))
        outp = ctx.enter_context(tc.tile_pool(name="outp", bufs=8))
        psum = ctx.enter_context(tc.psum_pool(name="psum", bufs=8))

        nu_v = nu.rearrange("(h p t) k -> h t p k", p=P, t=4)
        out_v = out.rearrange("(h p t) w -> h t p w", p=P, t=4)
        sens_v = sens.rearrange("(g p t) w -> g p t w", p=P, t=4)
        drdp_v = drdp.rearrange("(g p t) w -> g p t w", p=P, t=4)

        ident = keep.tile([P, P], F32, name="ident")
        gs_raw = keep.tile([P, GS, C], U8, name="gs_raw", align_bytes=64)
        gs = keep.tile([P, GS, C], U8, name="gs", align_bytes=64)
        unit_bf = keep.tile([P, M], BF16, name="unit_bf")
        unit_f = keep.tile([P, M], F32, name="unit_f")
        g_raw = [keep.tile([P, C], I32, name=f"g_raw{g}", align_bytes=64) for g in range(GS)]
        g_w = [keep.tile([P, C], I32, name=f"g_w{g}", align_bytes=64) for g in range(GS)]
        nu_raw = [keep.tile([P, R], BF16, name=f"nu_raw{i}", align_bytes=64) for i in range(M)]
        nu_c = [keep.tile([P, GD * P], I32, name=f"nu_c{i}", align_bytes=64) for i in range(M)]
        nu_s = [keep.tile([P, GD * P], U8, name=f"nu_s{i}", align_bytes=64) for i in range(M)]

        raw = {}
        codes = {}
        scales = {}
        for kind, passes in (("s", GS), ("d", GD)):
            for g in range(passes):
                a = keep.tile([P, 4, W], BF16, name=f"{kind}_raw{g}a", align_bytes=64)
                b = keep.tile([P, 4, 2 * W], BF16, name=f"{kind}_raw{g}b", align_bytes=64)
                raw[kind, g, 0] = a[:]
                raw[kind, g, 1] = b[:, :, 0:W]
                raw[kind, g, 2] = b[:, :, W : 2 * W]
                raw[kind, g, "b"] = b[:]
                for j in range(3):
                    codes[kind, g, j] = keep.tile([P, W], I32, name=f"{kind}_c{g}{j}", align_bytes=64)
                    scales[kind, g, j] = keep.tile([P, W], U8, name=f"{kind}_s{g}{j}", align_bytes=64)

        def load_small():
            for q in range(4):
                nc.sync.dma_start(
                    out=gs_raw[32 * q : 32 * q + 4, :, :].bitcast(I32),
                    in_=jac_scales[:, 4 * q : 4 * q + 4, :].rearrange("g r n -> r g n").bitcast(I32),
                )
            nc.sync.dma_start(out=unit_bf[:].rearrange("p (h t) -> p h t", t=4), in_=unit.rearrange("(h p t) -> p h t", p=P, t=4))

        def load(item):
            kind = item[0]
            if kind == "nu":
                i = item[1]
                parts = SPLIT0 if i == 0 else 1
                for c in range(parts):
                    cols = slice(c * R // parts, (c + 1) * R // parts)
                    nc.sync.dma_start(out=nu_raw[i][:, cols], in_=nu_v[i // 4, i % 4][:, cols])
            elif kind == "G":
                g = item[1]
                nc.sync.dma_start(out=g_raw[g][:], in_=jac_words[g].rearrange("p n t -> p (n t)").bitcast(I32))
            else:
                g, j = item[1], item[2]
                src = sens_v if kind == "s" else drdp_v
                if j == 0:
                    nc.sync.dma_start(out=raw[kind, g, 0], in_=src[g][:, :, 0:W])
                elif j == 1:
                    nc.sync.dma_start(out=raw[kind, g, "b"], in_=src[g][:, :, W : 3 * W])

        grouped = {}

        def front(item):
            kind = item[0]
            if kind == "nu":
                i = item[1]
                x = stage.tile([P, GD, P, 4], BF16, name="grouped", align_bytes=64)
                grouped[item] = x[:].rearrange("p g r t -> p (g r t)")
                words = nu_raw[i][:].bitcast(F32)
                xw = x[:].rearrange("p g r t -> p (g r t)").bitcast(F32)
                banks = []
                for half in range(2):
                    bank = psum.tile([P, W], F32, name="tbank", bufs=8 - OPEN)
                    banks.append(bank)
                    for gg in range(2):
                        for u in range(2):
                            base = 256 * (2 * half + gg) + u
                            nc.tensor.transpose(
                                bank[:, (2 * gg + u) * P : (2 * gg + u + 1) * P],
                                words[:, base : base + 255 : 2],
                                ident[:],
                            )
                for half in range(2):
                    src = banks[half][:].rearrange("p (g u r) -> p g r u", g=2, u=2)
                    dst = xw[:, W * half : W * (half + 1)].rearrange("p (g r u) -> p g r u", g=2, u=2)
                    if half in S_BANKS:
                        nc.scalar.copy(out=dst, in_=src)
                    else:
                        nc.vector.tensor_copy(out=dst, in_=src)
            elif kind == "G":
                g = item[1]
                nc.vector.tensor_copy(
                    out=g_w[g][:].rearrange("p (h t m) -> p h t m", t=4, m=P),
                    in_=g_raw[g][:].rearrange("p (h m t) -> p h t m", t=4, m=P),
                )
                if g == 0:
                    nc.vector.tensor_copy(
                        out=gs[:].rearrange("p g (h t m) -> p (g h) t m", t=4, m=P),
                        in_=gs_raw[:].rearrange("p g (h m t) -> p (g h) t m", t=4, m=P),
                    )
            else:
                kind, g, j = item
                x = stage.tile([P, W, 4], BF16, name="grouped", align_bytes=64)
                grouped[item] = x[:].rearrange("p w t -> p (w t)")
                src = raw[kind, g, j].rearrange("p t w -> p w t")
                v = V_WIDE if j else V_S0 if kind == "s" else V_D0
                nc.scalar.activation(out=x[:, v:W, :], in_=src[:, v:W, :], func=ACT.Copy, scale=0.5)
                nc.vector.tensor_scalar(out=x[:, 0:v, :], in0=src[:, 0:v, :], scalar1=0.5, scalar2=None, op0=ALU.mult)

        def middle(item):
            if item[0] == "nu":
                c, s = nu_c[item[1]], nu_s[item[1]]
            elif item[0] == "G":
                return
            else:
                c, s = codes[item], scales[item]
            nc.vector.quantize_mx(out=c[:].bitcast(E4M3), scales=s[:], in_=grouped[item])

        done = set()
        left = {}
        acc = {}
        todo = [(i, j) for j in range(3) for i in range(M)]
        opened = []
        finished = []

        def one_pass(i, j, step):
            kind, g = step
            n = len(left[i, j])
            if kind == "s":
                lt, ls = g_w[g][:, i * P : (i + 1) * P].bitcast(E5M2), gs[:, g, i * P : (i + 1) * P]
            else:
                lt, ls = nu_c[i][:, g * P : (g + 1) * P].bitcast(E4M3), nu_s[i][:, g * P : (g + 1) * P]
            nc.tensor.matmul_mx(
                out=acc[i, j][:],
                lhsT=lt,
                lhsT_scale=ls,
                rhs=codes[kind, g, j][:].bitcast(E4M3),
                rhs_scale=scales[kind, g, j][:],
                start=(n == GS + GD),
                stop=(n == 1),
            )
            left[i, j].remove(step)

        def ready(i, j, step):
            kind, g = step
            need = ("G", g) if kind == "s" else ("nu", i)
            return need in done and (kind, g, j) in done

        def back(item):
            done.add(item)
            progress = True
            while progress:
                progress = False
                while todo and len(opened) < OPEN and any(ready(*todo[0], s) for s in STEPS):
                    grp = todo.pop(0)
                    acc[grp] = psum.tile([P, W], F32, name="acc", bufs=OPEN)
                    left[grp] = list(STEPS)
                    opened.append(grp)
                for s in STEPS:
                    for grp in list(opened):
                        if s in left[grp] and ready(*grp, s):
                            one_pass(*grp, s)
                            if not left[grp]:
                                opened.remove(grp)
                                finished.append(grp)
                                flush(1)
                                progress = True

        def flush(keep_last):
            while len(finished) > keep_last:
                i, j = finished.pop(0)
                h, t = i // 4, i % 4
                o = outp.tile([P, W], F32, name="o")
                cols = slice(j * W, (j + 1) * W)
                nc.vector.scalar_tensor_tensor(
                    out=o[:],
                    in0=raw["s", h, j][:, t, :],
                    scalar=unit_f[:, i : i + 1],
                    in1=acc[i, j][:],
                    op0=ALU.mult,
                    op1=ALU.add,
                )
                nc.sync.dma_start(out=out_v[h, t][:, cols], in_=o[:])

        STEPS = [("s", g) for g in range(GS)] + [("d", g) for g in range(GD)]
        items = ITEMS1 + [(k, g, j) for j in (1, 2) for k, n in (("s", GS), ("d", GD)) for g in range(n)]

        make_identity(nc, ident[:])
        nc.vector.memset(gs_raw[:].rearrange("p g n -> p (g n)").bitcast(I32), 0)
        ahead = 10
        for n, item in enumerate(items[:ahead]):
            load(item)
            if n == 1:
                load_small()
        for n, item in enumerate(items):
            if n + ahead < len(items):
                load(items[n + ahead])
            front(item)
            if n == 0:
                nc.vector.tensor_copy(out=unit_f[:], in_=unit_bf[:])
            if n >= 1:
                middle(items[n - 1])
            flush(0)
            if n >= 2:
                back(items[n - 2])
        middle(items[-1])
        flush(0)
        back(items[-2])
        flush(0)
        back(items[-1])
        flush(0)
